import numpy as np
import ml_dtypes


def mxq(x, axis, fmt="e4m3"):
    dtype, down = {"e4m3": (ml_dtypes.float8_e4m3fn, 7), "e5m2": (ml_dtypes.float8_e5m2, 14)}[fmt]
    v = np.moveaxis(np.asarray(x, np.float32).astype(ml_dtypes.bfloat16).astype(np.float64), axis, -1)
    blocks = v.reshape(v.shape[:-1] + (-1, 32))
    amax = np.abs(blocks).max(-1, keepdims=True)
    byte = np.maximum(np.where(amax > 0, np.frexp(amax)[1] - 1 + 127, 0) - down, 1)
    scale = np.exp2(byte - 127.0)
    codes = (blocks / scale).astype(np.float32).astype(dtype).astype(np.float64)
    return np.moveaxis((codes * scale).reshape(v.shape), -1, axis)


WIDE = False


def mx_kscale(k):
    if not WIDE:
        return np.ones(k)
    levels = np.array([30, -30])
    if k % 512:
        return np.exp2(np.random.permutation(np.resize(levels, k // 32))).repeat(32)
    a = np.empty((k // 512, 16))
    for p in range(k // 512):
        a[p, :8] = np.random.permutation(np.resize(levels, 8))
        for g in range(8):
            far = levels[np.abs(levels - a[p, g]) >= 10]
            a[p, g + 8] = far[np.random.randint(len(far))]
    return np.exp2(a.ravel()).repeat(32)


BF16 = ml_dtypes.bfloat16


def bf(x):
    return np.asarray(x, np.float32).astype(BF16)


def f64(x):
    return np.asarray(x).astype(np.float64)


E2M1 = np.array([0.0, 0.5, 1.0, 1.5, 2.0, 3.0, 4.0, 6.0, -0.0, -0.5, -1.0, -1.5, -2.0, -3.0, -4.0, -6.0])


def pack_weight(w, fmt):
    k, n = w.shape
    w = f64(bf(w)).reshape(k // 32, 32, n)
    amax = np.abs(w).max(1)
    if fmt in ("e4m3", "e5m2"):
        byte = np.frexp(amax)[1] - 1 + 127 - (7 if fmt == "e4m3" else 14)
    else:
        mant, ex = np.frexp(amax / 6.0)
        byte = np.where(mant > 0.5, ex, ex - 1) + 127
    byte = np.clip(np.where(amax > 0, byte, 1), 1, 254)
    scaled = (w * np.exp2(127.0 - byte)[:, None, :]).reshape(k, n).astype(np.float32)
    by_word = np.ascontiguousarray(scaled.reshape(k // 512, 128, 4, n).transpose(0, 1, 3, 2))
    if fmt in ("e4m3", "e5m2"):
        words = by_word.astype(ml_dtypes.float8_e4m3fn if fmt == "e4m3" else ml_dtypes.float8_e5m2).view(np.uint8)
    else:
        c = by_word.astype(ml_dtypes.float4_e2m1fn).view(np.uint8) & 0xF
        words = c[..., 0::2] | (c[..., 1::2] << 4)
    return np.ascontiguousarray(words), np.ascontiguousarray(byte.astype(np.uint8).reshape(k // 512, 16, n))


def unpack_weight(words, scales, fmt):
    g, p, n, _ = words.shape
    if fmt in ("e4m3", "e5m2"):
        vals = np.ascontiguousarray(words).view(ml_dtypes.float8_e4m3fn if fmt == "e4m3" else ml_dtypes.float8_e5m2).astype(np.float64)
    else:
        nib = np.empty((g, p, n, 4), np.uint8)
        nib[..., 0::2] = words & 0xF
        nib[..., 1::2] = words >> 4
        vals = E2M1[nib]
    vals = vals * np.repeat(np.exp2(scales.astype(np.float64) - 127.0), 8, axis=1)[..., None]
    return vals.transpose(0, 1, 3, 2).reshape(g * 512, n)

def planes(Y):
    n, m = Y.shape
    b = f64(bf(Y)).reshape(n // 32, 32, m)
    amax = np.abs(b).max(1)
    byte = np.clip(np.where(amax > 0, np.frexp(amax)[1] - 1 + 127 - 7, 1), 1, 254)
    codes = (b * np.exp2(127.0 - byte)[:, None, :]).reshape(n, m).astype(np.float32).astype(ml_dtypes.float8_e4m3fn).view(np.uint8)
    words = codes.reshape(n // 512, 128, 4, m).transpose(0, 1, 3, 2)
    return np.ascontiguousarray(words), np.ascontiguousarray(byte.astype(np.uint8).reshape(n // 512, 16, m))


NC, NV, NB = 2048, 1536, 1024


def noise(*shape):
    return np.random.randn(*shape)

def setup_inputs():
    s = mx_kscale(NC)
    rho = np.exp(0.5 * noise(NC))
    z = noise(NC, NB) * np.exp(0.7 * noise(NC, NB))
    lam = noise(NC, NB) * np.exp(0.5 * noise(NC, NB))
    v = rho[:, None] * z - lam
    v_words, v_scales = pack_weight(v * s[:, None], "e5m2")
    a = 0.4 * noise(NC, NV) / np.sqrt(NC)
    return {
        "v_words": v_words,
        "v_scales": v_scales,
        "a": bf(a / s[:, None]),
        "c": bf(0.5 * noise(NV, NB)),
        "d": bf(np.exp(0.7 * noise(NV))),
        "sigma": bf(0.6 * np.exp(0.3 * noise(NV))),
        "x": bf(noise(NV, NB)),
    }

def reference(v_words, v_scales, a, c, d, sigma, x):
    V = unpack_weight(v_words, v_scales, "e5m2")
    A = mxq(f64(a), 0, "e4m3")
    r = A.T @ V
    y = f64(d)[:, None] * (r - f64(c)) + f64(sigma)[:, None] * f64(x)
    Y = y.reshape(NV, NB)
    words, scales = planes(Y)
    return y, words, scales

@@ -1,0 +1,302 @@
+from contextlib import ExitStack
+
+import concourse.mybir as mybir
+
+NC, NV, NB = 2048, 1536, 1024
+FLOPS = 2 * NC * NV * NB
+
+F32 = mybir.dt.float32
+BF16 = mybir.dt.bfloat16
+I32 = mybir.dt.int32
+U32 = mybir.dt.uint32
+U8 = mybir.dt.uint8
+E4M3X4 = mybir.dt.float8_e4m3fn_x4
+E5M2X4 = mybir.dt.float8_e5m2_x4
+ALU = mybir.AluOpType
+COPY = mybir.ActivationFunctionType.Copy
+
+P = 128
+PACK = 4
+SPAN = P * PACK
+PASSES = NC // SPAN
+GROUPS = NV // SPAN
+HALF = 512
+QUARTER = 256
+STAGES = 4
+VECTOR, SCALAR = "vector", "scalar"
+
+
+def tile_splitting_qp_kkt_rhs_k2_kernel(tc, v_words, v_scales, a, c, d, sigma, x, out_0, out_1, out_2):
+    nc = tc.nc
+    with ExitStack() as ctx:
+        sb = ctx.enter_context(tc.tile_pool(name="sb", bufs=1))
+        ps = ctx.enter_context(tc.psum_pool(name="ps", bufs=1))
+
+        def tile(name, shape, dtype):
+            return sb.tile(shape, dtype, name=name, align_bytes=64)
+
+        shared = tile("shared", [P, 8192], BF16)
+        wide = [tile("a_wide%d" % k, [P, PACK, 2 * SPAN], BF16) for k in range(PASSES)]
+        a_raw = [
+            [shared[:, 2048 * k : 2048 * (k + 1)].rearrange("p (j c) -> p j c", j=PACK) for k in range(PASSES)],
+            [wide[k][:, :, 0:SPAN] for k in range(PASSES)],
+            [wide[k][:, :, SPAN : 2 * SPAN] for k in range(PASSES)],
+        ]
+        stage = [tile("a_stage%d" % i, [P, SPAN * PACK], BF16) for i in range(STAGES)]
+        stage_index = {}
+        a_codes = [[tile("a_codes%d_%d" % (g, k), [P, SPAN], U32) for k in range(PASSES)] for g in range(GROUPS)]
+        a_scales = [[tile("a_scales%d_%d" % (g, k), [P, SPAN], U8) for k in range(PASSES)] for g in range(GROUPS)]
+        v_codes = [tile("v_codes%d" % h, [P, PASSES, HALF], U32) for h in range(2)]
+        v_plane = [tile("v_plane%d" % h, [P, PASSES, HALF], U8) for h in range(2)]
+        x_sb = [tile("x%d" % g, [P, PACK, NB], BF16)[:] for g in range(2)]
+        c_sb = [tile("c%d" % g, [P, PACK, NB], BF16)[:] for g in range(2)]
+        x_sb.append(shared[:, 0:4096].rearrange("p (t m) -> p t m", t=PACK))
+        c_sb.append(shared[:, 4096:8192].rearrange("p (t m) -> p t m", t=PACK))
+        y = [tile("y%d" % g, [P, PACK, NB], F32) for g in range(GROUPS)]
+        y_bf = [tile("y_bf%d" % h, [P, HALF * PACK], BF16) for h in range(2)]
+        y_codes = [tile("y_codes%d" % g, [P, NB], U32) for g in range(GROUPS)]
+        y_plane = [tile("y_plane%d" % g, [P, NB], U8) for g in range(GROUPS)]
+        d_bf = tile("d_bf", [P, GROUPS, PACK], BF16)
+        sigma_bf = tile("sigma_bf", [P, GROUPS * PACK], BF16)
+        sigma_f = tile("sigma_f", [P, GROUPS * PACK], F32)
+        bank = [[ps.tile([P, HALF], F32, name="bank%d_%d" % (h, t)) for t in range(PACK)] for h in range(2)]
+
+        def rows(ap, g):
+            return ap[g * SPAN : (g + 1) * SPAN, :].rearrange("(p t) m -> p t m", t=PACK)
+
+        def load_a(g0, g1, k):
+            src = a[k * SPAN : (k + 1) * SPAN, g0 * SPAN : g1 * SPAN].rearrange("(p j) c -> p j c", j=PACK)
+            nc.sync.dma_start(out=a_raw[g0][k] if g1 == g0 + 1 else wide[k][:], in_=src)
+
+        v_bytes = v_words.rearrange("k p n t -> p k (n t)")
+
+        def load_v(h, k0, k1):
+            src = v_bytes[:, k0:k1, h * HALF * PACK : (h + 1) * HALF * PACK].bitcast(I32)
+            nc.sync.dma_start(out=v_codes[h][:, k0:k1, :].bitcast(I32), in_=src)
+
+        def load_v_scales(h):
+            src = v_scales.rearrange("k (q r) n -> r q k n", r=4)
+            for r in range(4):
+                nc.sync.dma_start(
+                    out=v_plane[h][r:P:32, :, :].bitcast(I32),
+                    in_=src[r][:, :, h * HALF : (h + 1) * HALF].bitcast(I32),
+                )
+
+        def load_x(g, t0, t1, m0, m1):
+            nc.sync.dma_start(out=x_sb[g][:, t0:t1, m0:m1], in_=rows(x, g)[:, t0:t1, m0:m1])
+
+        def load_c(g, t0, t1, m0, m1):
+            nc.sync.dma_start(out=c_sb[g][:, t0:t1, m0:m1], in_=rows(c, g)[:, t0:t1, m0:m1])
+
+        def copy(engine, dst, src):
+            if engine == VECTOR:
+                nc.vector.tensor_copy(out=dst, in_=src)
+            else:
+                nc.scalar.copy(out=dst, in_=src)
+
+        def stage_of(g, k):
+            return stage[stage_index.setdefault((g, k), len(stage_index) % STAGES)]
+
+        def lay_a(g, k, pair, engine):
+            src = a_raw[g][k].rearrange("p j (u i t) -> p u j i t", i=2, t=PACK)
+            dst = stage_of(g, k)[:].rearrange("p (t u i j) -> p u j i t", t=PACK, i=2, j=PACK)
+            ts = slice(2 * pair, 2 * pair + 2)
+            copy(engine, dst[:, :, :, :, ts], src[:, :, :, :, ts])
+
+        def quantize_a(g, k):
+            nc.vector.quantize_mx(
+                out=a_codes[g][k][:].bitcast(E4M3X4), scales=a_scales[g][k][:], in_=stage_of(g, k)[:]
+            )
+
+        def multiply(g, h, t, k):
+            cols = slice(t * P, (t + 1) * P)
+            nc.tensor.matmul_mx(
+                out=bank[h][t][:],
+                lhsT=a_codes[g][k][:, cols].bitcast(E4M3X4),
+                lhsT_scale=a_scales[g][k][:, cols],
+                rhs=v_codes[h][:, k, :].bitcast(E5M2X4),
+                rhs_scale=v_plane[h][:, k, :],
+                start=(k == 0),
+                stop=(k == PASSES - 1),
+            )
+
+        def scale_x(g, t, m0, m1):
+            col = g * PACK + t
+            nc.scalar.activation(
+                out=y[g][:, t, m0:m1], in_=x_sb[g][:, t, m0:m1], func=COPY, scale=sigma_f[:, col : col + 1]
+            )
+
+        def add_cost(g, t, m0, m1):
+            nc.vector.scalar_tensor_tensor(
+                out=y[g][:, t, m0:m1], in0=c_sb[g][:, t, m0:m1], scalar=d_bf[:, g, t : t + 1],
+                in1=y[g][:, t, m0:m1], op0=ALU.mult, op1=ALU.subtract,
+            )
+
+        def add_product(g, t, m0, m1):
+            h = m0 // HALF
+            nc.vector.scalar_tensor_tensor(
+                out=y[g][:, t, m0:m1], in0=bank[h][t][:, m0 - h * HALF : m1 - h * HALF],
+                scalar=d_bf[:, g, t : t + 1], in1=y[g][:, t, m0:m1], op0=ALU.mult, op1=ALU.subtract,
+            )
+
+        def y_stage(m0, m1):
+            h = m0 // HALF
+            return y_bf[h][:, (m0 - h * HALF) * PACK : (m1 - h * HALF) * PACK]
+
+        def lay_y(g, m0, m1, engine):
+            src = y[g][:, :, m0:m1].rearrange("p t (u i) -> p u t i", i=4)
+            dst = y_stage(m0, m1).rearrange("p (u i t) -> p u t i", i=4, t=PACK)
+            copy(engine, dst, src)
+
+        def quantize_y(g, m0, m1):
+            nc.vector.quantize_mx(
+                out=y_codes[g][:, m0:m1].bitcast(E4M3X4), scales=y_plane[g][:, m0:m1], in_=y_stage(m0, m1)
+            )
+
+        def store_y(g, m0, m1):
+            nc.sync.dma_start(out=rows(out_0, g)[:, :, m0:m1], in_=y[g][:, :, m0:m1])
+
+        def store_codes(g, m0, m1):
+            dst = out_1[g].rearrange("p m t -> p (m t)")[:, m0 * PACK : m1 * PACK].bitcast(I32)
+            nc.sync.dma_start(out=dst, in_=y_codes[g][:, m0:m1].bitcast(I32))
+
+        def store_scales(g):
+            dst = out_2[g].rearrange("(q r) m -> r q m", r=4)
+            for r in range(4):
+                nc.sync.dma_start(out=dst[r].bitcast(I32), in_=y_plane[g][r:P:32, :].bitcast(I32))
+
+        def each_t(step, first, *rest):
+            for t in range(PACK):
+                step(first, t, *rest)
+
+        ctx.enter_context(tc.manual_schedule())
+
+        for h in range(2):
+            nc.vector.memset(v_plane[h][:].bitcast(U32), 0)
+        nc.scalar.dma_start(
+            out=sigma_bf[:].rearrange("p (g t) -> p g t", t=PACK),
+            in_=sigma.rearrange("(g p t) -> p g t", p=P, t=PACK),
+        )
+        nc.scalar.dma_start(out=d_bf[:], in_=d.rearrange("(g p t) -> p g t", p=P, t=PACK))
+        nc.scalar.activation(out=sigma_f[:], in_=sigma_bf[:], func=COPY)
+
+        load_a(0, 1, 0)
+        load_a(0, 1, 1)
+        load_v_scales(0)
+        load_v(0, 0, 1)
+        load_a(0, 1, 2)
+        load_v(0, 1, 2)
+        load_a(0, 1, 3)
+        load_x(0, 0, 2, 0, HALF)
+        load_c(0, 0, 2, 0, HALF)
+        load_v(0, 2, 3)
+        load_x(0, 2, 4, 0, HALF)
+        load_c(0, 2, 4, 0, HALF)
+        load_v(0, 3, 4)
+        load_x(0, 0, 4, HALF, NB)
+        load_v_scales(1)
+        load_v(1, 0, 2)
+        load_c(0, 0, 4, HALF, NB)
+        load_v(1, 2, 4)
+        load_a(1, 3, 0)
+        load_a(1, 3, 1)
+        load_a(1, 2, 2)
+        load_a(1, 2, 3)
+        load_x(1, 0, 4, 0, NB)
+        load_c(1, 0, 4, 0, NB)
+        load_a(2, 3, 2)
+        load_a(2, 3, 3)
+
+        for k in range(PASSES):
+            lay_a(0, k, 1, SCALAR)
+            lay_a(0, k, 0, VECTOR)
+            if k == 1:
+                quantize_a(0, 0)
+            if k >= 1:
+                quantize_a(0, k)
+        load_x(2, 0, 4, 0, NB)
+        load_c(2, 0, 4, 0, NB)
+        for k in range(PASSES):
+            each_t(lambda h, t: multiply(0, h, t, k), 0)
+        for k in range(2):
+            each_t(lambda h, t: multiply(0, h, t, k), 1)
+        for t in range(PACK):
+            for k in range(2, PASSES):
+                multiply(0, 1, t, k)
+        each_t(scale_x, 0, 0, HALF)
+        each_t(add_cost, 0, 0, HALF)
+        each_t(scale_x, 0, HALF, NB)
+        each_t(add_product, 0, 0, HALF)
+        lay_y(0, 0, HALF, SCALAR)
+        each_t(add_cost, 0, HALF, NB)
+        quantize_y(0, 0, HALF)
+        each_t(add_product, 0, HALF, NB)
+
+        lay_a(1, 0, 1, SCALAR)
+        lay_a(2, 0, 1, SCALAR)
+        lay_y(0, HALF, NB, SCALAR)
+        lay_a(1, 0, 0, VECTOR)
+        lay_a(2, 0, 0, VECTOR)
+        quantize_a(1, 0)
+        lay_a(1, 1, 1, SCALAR)
+        lay_a(1, 1, 0, VECTOR)
+        quantize_a(2, 0)
+        lay_a(1, 2, 1, SCALAR)
+        lay_a(1, 2, 0, VECTOR)
+        quantize_y(0, HALF, NB)
+        quantize_a(1, 1)
+        lay_a(1, 3, 1, SCALAR)
+        lay_a(1, 3, 0, VECTOR)
+        quantize_a(1, 2)
+        lay_a(2, 1, 0, VECTOR)
+        quantize_a(1, 3)
+        for k in range(PASSES):
+            for h in range(2):
+                each_t(lambda h, t: multiply(1, h, t, k), h)
+        store_y(0, 0, NB)
+        store_codes(0, 0, NB)
+        store_scales(0)
+
+        each_t(scale_x, 1, 0, NB)
+        lay_a(2, 1, 1, SCALAR)
+        each_t(add_cost, 1, 0, NB)
+        lay_a(2, 2, 1, SCALAR)
+        lay_a(2, 2, 0, SCALAR)
+        quantize_a(2, 1)
+        lay_a(2, 3, 1, SCALAR)
+        lay_a(2, 3, 0, SCALAR)
+        each_t(add_product, 1, 0, HALF)
+        store_y(1, 0, HALF)
+        quantize_a(2, 2)
+        each_t(scale_x, 2, 0, HALF)
+        each_t(add_product, 1, HALF, NB)
+        store_y(1, HALF, NB)
+        quantize_a(2, 3)
+        for h in range(2):
+            for t in range(PACK):
+                for k in range(PASSES):
+                    multiply(2, h, t, k)
+        lay_y(1, 0, HALF, SCALAR)
+        each_t(add_cost, 2, 0, HALF)
+        each_t(scale_x, 2, HALF, NB)
+        quantize_y(1, 0, HALF)
+        lay_y(1, HALF, NB, SCALAR)
+        each_t(add_product, 2, 0, HALF)
+        store_y(2, 0, HALF)
+        lay_y(2, 0, HALF, SCALAR)
+        each_t(add_cost, 2, HALF, NB)
+        quantize_y(1, HALF, NB)
+        store_codes(1, 0, NB)
+        store_scales(1)
+        each_t(add_product, 2, HALF, HALF + QUARTER)
+        store_y(2, HALF, HALF + QUARTER)
+        lay_y(2, HALF, HALF + QUARTER, SCALAR)
+        each_t(add_product, 2, HALF + QUARTER, NB)
+        store_y(2, HALF + QUARTER, NB)
+        quantize_y(2, 0, HALF)
+        store_codes(2, 0, HALF)
+        lay_y(2, HALF + QUARTER, NB, VECTOR)
+        quantize_y(2, HALF, HALF + QUARTER)
+        quantize_y(2, HALF + QUARTER, NB)
+        store_codes(2, HALF, NB)
+        store_scales(2)

@@ -22,8 +22,8 @@ PASSES = NC // SPAN
 GROUPS = NV // SPAN
 HALF = 512
 QUARTER = 256
-STAGES = 4
-VECTOR, SCALAR = "vector", "scalar"
+STAGES = 6
+VECTOR, SCALAR, GPSIMD = "vector", "scalar", "gpsimd"
 
 
 def tile_splitting_qp_kkt_rhs_k2_kernel(tc, v_words, v_scales, a, c, d, sigma, x, out_0, out_1, out_2):
@@ -32,15 +32,14 @@ def tile_splitting_qp_kkt_rhs_k2_kernel(tc, v_words, v_scales, a, c, d, sigma, x
         sb = ctx.enter_context(tc.tile_pool(name="sb", bufs=1))
         ps = ctx.enter_context(tc.psum_pool(name="ps", bufs=1))
 
-        def tile(name, shape, dtype):
-            return sb.tile(shape, dtype, name=name, align_bytes=64)
+        def tile(name, shape, dtype, tag=None):
+            return sb.tile(shape, dtype, name=name, tag=tag or name, align_bytes=64)
 
         shared = tile("shared", [P, 8192], BF16)
-        wide = [tile("a_wide%d" % k, [P, PACK, 2 * SPAN], BF16) for k in range(PASSES)]
         a_raw = [
             [shared[:, 2048 * k : 2048 * (k + 1)].rearrange("p (j c) -> p j c", j=PACK) for k in range(PASSES)],
-            [wide[k][:, :, 0:SPAN] for k in range(PASSES)],
-            [wide[k][:, :, SPAN : 2 * SPAN] for k in range(PASSES)],
+            [tile("a_raw1_%d" % k, [P, PACK, SPAN], BF16)[:] for k in range(PASSES)],
+            [tile("a_raw2_%d" % k, [P, PACK, SPAN], BF16)[:] for k in range(PASSES)],
         ]
         stage = [tile("a_stage%d" % i, [P, SPAN * PACK], BF16) for i in range(STAGES)]
         stage_index = {}
@@ -48,17 +47,16 @@ def tile_splitting_qp_kkt_rhs_k2_kernel(tc, v_words, v_scales, a, c, d, sigma, x
         a_scales = [[tile("a_scales%d_%d" % (g, k), [P, SPAN], U8) for k in range(PASSES)] for g in range(GROUPS)]
         v_codes = [tile("v_codes%d" % h, [P, PASSES, HALF], U32) for h in range(2)]
         v_plane = [tile("v_plane%d" % h, [P, PASSES, HALF], U8) for h in range(2)]
-        x_sb = [tile("x%d" % g, [P, PACK, NB], BF16)[:] for g in range(2)]
-        c_sb = [tile("c%d" % g, [P, PACK, NB], BF16)[:] for g in range(2)]
-        x_sb.append(shared[:, 0:4096].rearrange("p (t m) -> p t m", t=PACK))
-        c_sb.append(shared[:, 4096:8192].rearrange("p (t m) -> p t m", t=PACK))
-        y = [tile("y%d" % g, [P, PACK, NB], F32) for g in range(GROUPS)]
-        y_bf = [tile("y_bf%d" % h, [P, HALF * PACK], BF16) for h in range(2)]
+        xc = [tile("xc%d" % g, [P, 2, PACK, NB], BF16) for g in range(2)]
+        x_sb = [xc[0][:, 0], xc[1][:, 0], shared[:, 0:4096].rearrange("p (t m) -> p t m", t=PACK)]
+        c_sb = [xc[0][:, 1], xc[1][:, 1], shared[:, 4096:8192].rearrange("p (t m) -> p t m", t=PACK)]
+        y = [tile("y%d" % g, [P, PACK, NB], F32) for g in range(2)]
+        y_bf = [tile("y_bf%d" % g, [P, NB * PACK], BF16) for g in range(GROUPS)]
         y_codes = [tile("y_codes%d" % g, [P, NB], U32) for g in range(GROUPS)]
-        y_plane = [tile("y_plane%d" % g, [P, NB], U8) for g in range(GROUPS)]
-        d_bf = tile("d_bf", [P, GROUPS, PACK], BF16)
-        sigma_bf = tile("sigma_bf", [P, GROUPS * PACK], BF16)
-        sigma_f = tile("sigma_f", [P, GROUPS * PACK], F32)
+        y_plane = tile("y_plane", [P, GROUPS, NB], U8)
+        d_bf = tile("d_bf", [P, GROUPS, 16], BF16)
+        sigma_bf = tile("sigma_bf", [P, GROUPS, 16], BF16)
+        sigma_f = tile("sigma_f", [P, GROUPS, PACK], F32)
         bank = [[ps.tile([P, HALF], F32, name="bank%d_%d" % (h, t)) for t in range(PACK)] for h in range(2)]
 
         def rows(ap, g):
@@ -66,7 +64,7 @@ def tile_splitting_qp_kkt_rhs_k2_kernel(tc, v_words, v_scales, a, c, d, sigma, x
 
         def load_a(g0, g1, k):
             src = a[k * SPAN : (k + 1) * SPAN, g0 * SPAN : g1 * SPAN].rearrange("(p j) c -> p j c", j=PACK)
-            nc.sync.dma_start(out=a_raw[g0][k] if g1 == g0 + 1 else wide[k][:], in_=src)
+            nc.sync.dma_start(out=a_raw[g0][k], in_=src)
 
         v_bytes = v_words.rearrange("k p n t -> p k (n t)")
 
@@ -120,11 +118,18 @@ def tile_splitting_qp_kkt_rhs_k2_kernel(tc, v_words, v_scales, a, c, d, sigma, x
                 stop=(k == PASSES - 1),
             )
 
-        def scale_x(g, t, m0, m1):
-            col = g * PACK + t
-            nc.scalar.activation(
-                out=y[g][:, t, m0:m1], in_=x_sb[g][:, t, m0:m1], func=COPY, scale=sigma_f[:, col : col + 1]
-            )
+        def scale_x(g, t, m0, m1, engine=SCALAR):
+            if g == len(y):
+                y.append(tile("y%d" % g, [P, PACK, NB], F32, tag="xc1"))
+            if engine == SCALAR:
+                nc.scalar.activation(
+                    out=y[g][:, t, m0:m1], in_=x_sb[g][:, t, m0:m1], func=COPY, scale=sigma_f[:, g, t : t + 1]
+                )
+            else:
+                nc.gpsimd.tensor_scalar(
+                    out=y[g][:, t, m0:m1], in0=x_sb[g][:, t, m0:m1], scalar1=sigma_f[:, g, t : t + 1],
+                    scalar2=0.0, op0=ALU.mult, op1=ALU.add,
+                )
 
         def add_cost(g, t, m0, m1):
             nc.vector.scalar_tensor_tensor(
@@ -139,18 +144,17 @@ def tile_splitting_qp_kkt_rhs_k2_kernel(tc, v_words, v_scales, a, c, d, sigma, x
                 scalar=d_bf[:, g, t : t + 1], in1=y[g][:, t, m0:m1], op0=ALU.mult, op1=ALU.subtract,
             )
 
-        def y_stage(m0, m1):
-            h = m0 // HALF
-            return y_bf[h][:, (m0 - h * HALF) * PACK : (m1 - h * HALF) * PACK]
+        def y_stage(g, m0, m1):
+            return y_bf[g][:, m0 * PACK : m1 * PACK]
 
         def lay_y(g, m0, m1, engine):
             src = y[g][:, :, m0:m1].rearrange("p t (u i) -> p u t i", i=4)
-            dst = y_stage(m0, m1).rearrange("p (u i t) -> p u t i", i=4, t=PACK)
+            dst = y_stage(g, m0, m1).rearrange("p (u i t) -> p u t i", i=4, t=PACK)
             copy(engine, dst, src)
 
         def quantize_y(g, m0, m1):
             nc.vector.quantize_mx(
-                out=y_codes[g][:, m0:m1].bitcast(E4M3X4), scales=y_plane[g][:, m0:m1], in_=y_stage(m0, m1)
+                out=y_codes[g][:, m0:m1].bitcast(E4M3X4), scales=y_plane[:, g, m0:m1], in_=y_stage(g, m0, m1)
             )
 
         def store_y(g, m0, m1):
@@ -160,135 +164,149 @@ def tile_splitting_qp_kkt_rhs_k2_kernel(tc, v_words, v_scales, a, c, d, sigma, x
             dst = out_1[g].rearrange("p m t -> p (m t)")[:, m0 * PACK : m1 * PACK].bitcast(I32)
             nc.sync.dma_start(out=dst, in_=y_codes[g][:, m0:m1].bitcast(I32))
 
-        def store_scales(g):
-            dst = out_2[g].rearrange("(q r) m -> r q m", r=4)
+        def store_scales(g0, g1):
+            dst = out_2[g0:g1].rearrange("g (q r) m -> r q g m", r=4)
             for r in range(4):
-                nc.sync.dma_start(out=dst[r].bitcast(I32), in_=y_plane[g][r:P:32, :].bitcast(I32))
+                nc.sync.dma_start(out=dst[r].bitcast(I32), in_=y_plane[r:P:32, g0:g1, :].bitcast(I32))
 
         def each_t(step, first, *rest):
             for t in range(PACK):
+                step(first, t, *rest)
+
+        def last_first(step, first, *rest):
+            for t in (3, 0, 1, 2):
                 step(first, t, *rest)
 
         ctx.enter_context(tc.manual_schedule())
 
         for h in range(2):
             nc.vector.memset(v_plane[h][:].bitcast(U32), 0)
-        nc.scalar.dma_start(
-            out=sigma_bf[:].rearrange("p (g t) -> p g t", t=PACK),
-            in_=sigma.rearrange("(g p t) -> p g t", p=P, t=PACK),
-        )
-        nc.scalar.dma_start(out=d_bf[:], in_=d.rearrange("(g p t) -> p g t", p=P, t=PACK))
-        nc.scalar.activation(out=sigma_f[:], in_=sigma_bf[:], func=COPY)
+        nc.scalar.dma_start(out=sigma_bf[:, :, 0:PACK], in_=sigma.rearrange("(g p t) -> p g t", p=P, t=PACK))
+        nc.scalar.activation(out=sigma_f[:], in_=sigma_bf[:, :, 0:PACK], func=COPY)
 
         load_a(0, 1, 0)
         load_a(0, 1, 1)
         load_v_scales(0)
-        load_v(0, 0, 1)
+        load_v(0, 0, 2)
         load_a(0, 1, 2)
-        load_v(0, 1, 2)
         load_a(0, 1, 3)
-        load_x(0, 0, 2, 0, HALF)
-        load_c(0, 0, 2, 0, HALF)
-        load_v(0, 2, 3)
-        load_x(0, 2, 4, 0, HALF)
-        load_c(0, 2, 4, 0, HALF)
-        load_v(0, 3, 4)
-        load_x(0, 0, 4, HALF, NB)
+        nc.sync.dma_start(out=d_bf[:, :, 0:PACK], in_=d.rearrange("(g p t) -> p g t", p=P, t=PACK))
+        load_x(0, 0, 2, 0, NB)
+        load_c(0, 0, 2, 0, NB)
+        load_v(0, 2, 4)
+        load_x(0, 2, 4, 0, NB)
+        load_c(0, 2, 4, 0, NB)
         load_v_scales(1)
         load_v(1, 0, 2)
-        load_c(0, 0, 4, HALF, NB)
+        load_x(1, 0, 2, 0, NB)
         load_v(1, 2, 4)
-        load_a(1, 3, 0)
-        load_a(1, 3, 1)
+        load_a(1, 2, 0)
+        load_a(1, 2, 1)
+        load_c(1, 0, 2, 0, NB)
         load_a(1, 2, 2)
         load_a(1, 2, 3)
-        load_x(1, 0, 4, 0, NB)
-        load_c(1, 0, 4, 0, NB)
-        load_a(2, 3, 2)
-        load_a(2, 3, 3)
+        load_x(1, 2, 4, 0, NB)
+        load_c(1, 2, 4, 0, NB)
 
         for k in range(PASSES):
             lay_a(0, k, 1, SCALAR)
             lay_a(0, k, 0, VECTOR)
-            if k == 1:
-                quantize_a(0, 0)
             if k >= 1:
-                quantize_a(0, k)
+                quantize_a(0, k - 1)
+        quantize_a(0, PASSES - 1)
+        load_a(2, 3, 0)
         load_x(2, 0, 4, 0, NB)
+        load_a(2, 3, 1)
+        load_a(2, 3, 2)
+        load_a(2, 3, 3)
         load_c(2, 0, 4, 0, NB)
-        for k in range(PASSES):
+        for k in range(2):
             each_t(lambda h, t: multiply(0, h, t, k), 0)
+        for t in range(PACK):
+            for k in range(2, PASSES):
+                multiply(0, 0, t, k)
         for k in range(2):
             each_t(lambda h, t: multiply(0, h, t, k), 1)
         for t in range(PACK):
             for k in range(2, PASSES):
                 multiply(0, 1, t, k)
-        each_t(scale_x, 0, 0, HALF)
-        each_t(add_cost, 0, 0, HALF)
-        each_t(scale_x, 0, HALF, NB)
-        each_t(add_product, 0, 0, HALF)
-        lay_y(0, 0, HALF, SCALAR)
-        each_t(add_cost, 0, HALF, NB)
-        quantize_y(0, 0, HALF)
+        each_t(scale_x, 0, 0, NB)
+        add_cost(0, 0, 0, NB)
+        add_cost(0, 1, 0, NB)
+        add_product(0, 0, 0, HALF)
+        add_product(0, 1, 0, HALF)
+        add_cost(0, 2, 0, NB)
+        add_cost(0, 3, 0, NB)
+        add_product(0, 2, 0, HALF)
+        add_product(0, 3, 0, HALF)
+        scale_x(1, 0, 0, NB)
+        scale_x(1, 1, 0, NB)
         each_t(add_product, 0, HALF, NB)
-
         lay_a(1, 0, 1, SCALAR)
-        lay_a(2, 0, 1, SCALAR)
-        lay_y(0, HALF, NB, SCALAR)
-        lay_a(1, 0, 0, VECTOR)
-        lay_a(2, 0, 0, VECTOR)
-        quantize_a(1, 0)
+        lay_a(1, 0, 0, SCALAR)
         lay_a(1, 1, 1, SCALAR)
         lay_a(1, 1, 0, VECTOR)
-        quantize_a(2, 0)
-        lay_a(1, 2, 1, SCALAR)
-        lay_a(1, 2, 0, VECTOR)
-        quantize_y(0, HALF, NB)
+        quantize_a(1, 0)
+        add_cost(1, 0, 0, NB)
         quantize_a(1, 1)
+        lay_a(1, 2, 1, SCALAR)
+        lay_a(1, 2, 0, SCALAR)
+        add_cost(1, 1, 0, NB)
         lay_a(1, 3, 1, SCALAR)
         lay_a(1, 3, 0, VECTOR)
         quantize_a(1, 2)
-        lay_a(2, 1, 0, VECTOR)
         quantize_a(1, 3)
-        for k in range(PASSES):
+        for k in range(PASSES - 1):
             for h in range(2):
                 each_t(lambda h, t: multiply(1, h, t, k), h)
-        store_y(0, 0, NB)
-        store_codes(0, 0, NB)
-        store_scales(0)
-
-        each_t(scale_x, 1, 0, NB)
-        lay_a(2, 1, 1, SCALAR)
-        each_t(add_cost, 1, 0, NB)
-        lay_a(2, 2, 1, SCALAR)
-        lay_a(2, 2, 0, SCALAR)
-        quantize_a(2, 1)
-        lay_a(2, 3, 1, SCALAR)
-        lay_a(2, 3, 0, SCALAR)
-        each_t(add_product, 1, 0, HALF)
-        store_y(1, 0, HALF)
-        quantize_a(2, 2)
-        each_t(scale_x, 2, 0, HALF)
-        each_t(add_product, 1, HALF, NB)
-        store_y(1, HALF, NB)
-        quantize_a(2, 3)
         for h in range(2):
-            for t in range(PACK):
-                for k in range(PASSES):
-                    multiply(2, h, t, k)
+            each_t(lambda h, t: multiply(1, h, t, 3), h)
+        scale_x(1, 2, 0, NB)
+        scale_x(1, 3, 0, NB)
+        add_cost(1, 2, 0, NB)
+        add_cost(1, 3, 0, NB)
+        each_t(scale_x, 2, 0, NB, GPSIMD)
+        each_t(add_product, 1, 0, HALF)
+        store_y(0, 0, NB)
+        last_first(add_product, 1, HALF, NB)
+        store_y(1, 0, HALF)
+        store_y(1, HALF, NB)
+        for k in range(4):
+            lay_a(2, k, 1, SCALAR)
+            lay_a(2, k, 0, SCALAR)
+        quantize_a(2, 0)
+        quantize_a(2, 1)
+        quantize_a(2, 2)
+        add_cost(2, 0, 0, HALF)
+        quantize_a(2, 3)
+        add_cost(2, 1, 0, HALF)
+        add_cost(2, 2, 0, HALF)
+        add_cost(2, 3, 0, HALF)
+        for k in range(3):
+            each_t(lambda h, t: multiply(2, h, t, k), 0)
+        last_first(lambda h, t: multiply(2, h, t, 3), 0)
+        for t in (3, 0, 1, 2):
+            for k in range(PASSES):
+                multiply(2, 1, t, k)
+        lay_y(0, 0, HALF, SCALAR)
+        lay_y(0, HALF, NB, SCALAR)
         lay_y(1, 0, HALF, SCALAR)
-        each_t(add_cost, 2, 0, HALF)
-        each_t(scale_x, 2, HALF, NB)
-        quantize_y(1, 0, HALF)
+        quantize_y(0, 0, HALF)
         lay_y(1, HALF, NB, SCALAR)
-        each_t(add_product, 2, 0, HALF)
+        last_first(add_product, 2, 0, HALF)
         store_y(2, 0, HALF)
+        quantize_y(0, HALF, NB)
+        store_codes(0, 0, NB)
         lay_y(2, 0, HALF, SCALAR)
-        each_t(add_cost, 2, HALF, NB)
+        add_cost(2, 0, HALF, NB)
+        add_cost(2, 1, HALF, NB)
+        quantize_y(1, 0, HALF)
+        add_cost(2, 2, HALF, NB)
+        add_cost(2, 3, HALF, NB)
         quantize_y(1, HALF, NB)
         store_codes(1, 0, NB)
-        store_scales(1)
-        each_t(add_product, 2, HALF, HALF + QUARTER)
+        store_scales(0, 2)
+        last_first(add_product, 2, HALF, HALF + QUARTER)
         store_y(2, HALF, HALF + QUARTER)
         lay_y(2, HALF, HALF + QUARTER, SCALAR)
         each_t(add_product, 2, HALF + QUARTER, NB)
@@ -299,4 +317,4 @@ def tile_splitting_qp_kkt_rhs_k2_kernel(tc, v_words, v_scales, a, c, d, sigma, x
         quantize_y(2, HALF, HALF + QUARTER)
         quantize_y(2, HALF + QUARTER, NB)
         store_codes(2, HALF, NB)
-        store_scales(2)
+        store_scales(2, 3)

@@ -118,37 +118,43 @@ def tile_splitting_qp_kkt_rhs_k2_kernel(tc, v_words, v_scales, a, c, d, sigma, x
                 stop=(k == PASSES - 1),
             )
 
+        def y_part(g, m0, m1):
+            if g < 2:
+                return y[g][:, :, m0:m1]
+            h = m0 // HALF
+            return y[g][:, h, :, m0 - h * HALF : m1 - h * HALF]
+
         def scale_x(g, t, m0, m1, engine=SCALAR):
             if g == len(y):
-                y.append(tile("y%d" % g, [P, PACK, NB], F32, tag="xc1"))
+                y.append(tile("y%d" % g, [P, 2, PACK, HALF], F32, tag="xc1"))
             if engine == SCALAR:
                 nc.scalar.activation(
-                    out=y[g][:, t, m0:m1], in_=x_sb[g][:, t, m0:m1], func=COPY, scale=sigma_f[:, g, t : t + 1]
+                    out=y_part(g, m0, m1)[:, t, :], in_=x_sb[g][:, t, m0:m1], func=COPY, scale=sigma_f[:, g, t : t + 1]
                 )
             else:
                 nc.gpsimd.tensor_scalar(
-                    out=y[g][:, t, m0:m1], in0=x_sb[g][:, t, m0:m1], scalar1=sigma_f[:, g, t : t + 1],
+                    out=y[g][:, :, t, :], in0=x_sb[g][:, t, :].rearrange("p (h m) -> p h m", h=2), scalar1=sigma_f[:, g, t : t + 1],
                     scalar2=0.0, op0=ALU.mult, op1=ALU.add,
                 )
 
         def add_cost(g, t, m0, m1):
             nc.vector.scalar_tensor_tensor(
-                out=y[g][:, t, m0:m1], in0=c_sb[g][:, t, m0:m1], scalar=d_bf[:, g, t : t + 1],
-                in1=y[g][:, t, m0:m1], op0=ALU.mult, op1=ALU.subtract,
+                out=y_part(g, m0, m1)[:, t, :], in0=c_sb[g][:, t, m0:m1], scalar=d_bf[:, g, t : t + 1],
+                in1=y_part(g, m0, m1)[:, t, :], op0=ALU.mult, op1=ALU.subtract,
             )
 
         def add_product(g, t, m0, m1):
             h = m0 // HALF
             nc.vector.scalar_tensor_tensor(
-                out=y[g][:, t, m0:m1], in0=bank[h][t][:, m0 - h * HALF : m1 - h * HALF],
-                scalar=d_bf[:, g, t : t + 1], in1=y[g][:, t, m0:m1], op0=ALU.mult, op1=ALU.subtract,
+                out=y_part(g, m0, m1)[:, t, :], in0=bank[h][t][:, m0 - h * HALF : m1 - h * HALF],
+                scalar=d_bf[:, g, t : t + 1], in1=y_part(g, m0, m1)[:, t, :], op0=ALU.mult, op1=ALU.subtract,
             )
 
         def y_stage(g, m0, m1):
             return y_bf[g][:, m0 * PACK : m1 * PACK]
 
         def lay_y(g, m0, m1, engine):
-            src = y[g][:, :, m0:m1].rearrange("p t (u i) -> p u t i", i=4)
+            src = y_part(g, m0, m1).rearrange("p t (u i) -> p u t i", i=4)
             dst = y_stage(g, m0, m1).rearrange("p (u i t) -> p u t i", i=4, t=PACK)
             copy(engine, dst, src)
 
@@ -158,16 +164,16 @@ def tile_splitting_qp_kkt_rhs_k2_kernel(tc, v_words, v_scales, a, c, d, sigma, x
             )
 
         def store_y(g, m0, m1):
-            nc.sync.dma_start(out=rows(out_0, g)[:, :, m0:m1], in_=y[g][:, :, m0:m1])
+            nc.sync.dma_start(out=rows(out_0, g)[:, :, m0:m1], in_=y_part(g, m0, m1))
 
         def store_codes(g, m0, m1):
             dst = out_1[g].rearrange("p m t -> p (m t)")[:, m0 * PACK : m1 * PACK].bitcast(I32)
             nc.sync.dma_start(out=dst, in_=y_codes[g][:, m0:m1].bitcast(I32))
 
-        def store_scales(g0, g1):
+        def store_scales(g0, g1, queue):
             dst = out_2[g0:g1].rearrange("g (q r) m -> r q g m", r=4)
             for r in range(4):
-                nc.sync.dma_start(out=dst[r].bitcast(I32), in_=y_plane[r:P:32, g0:g1, :].bitcast(I32))
+                queue.dma_start(out=dst[r].bitcast(I32), in_=y_plane[r:P:32, g0:g1, :].bitcast(I32))
 
         def each_t(step, first, *rest):
             for t in range(PACK):
@@ -305,7 +311,7 @@ def tile_splitting_qp_kkt_rhs_k2_kernel(tc, v_words, v_scales, a, c, d, sigma, x
         add_cost(2, 3, HALF, NB)
         quantize_y(1, HALF, NB)
         store_codes(1, 0, NB)
-        store_scales(0, 2)
+        store_scales(0, 2, nc.sync)
         last_first(add_product, 2, HALF, HALF + QUARTER)
         store_y(2, HALF, HALF + QUARTER)
         lay_y(2, HALF, HALF + QUARTER, SCALAR)
@@ -317,4 +323,4 @@ def tile_splitting_qp_kkt_rhs_k2_kernel(tc, v_words, v_scales, a, c, d, sigma, x
         quantize_y(2, HALF, HALF + QUARTER)
         quantize_y(2, HALF + QUARTER, NB)
         store_codes(2, HALF, NB)
-        store_scales(2, 3)
+        store_scales(2, 3, nc.scalar)

@@ -35,25 +35,31 @@ def tile_splitting_qp_kkt_rhs_k2_kernel(tc, v_words, v_scales, a, c, d, sigma, x
         def tile(name, shape, dtype, tag=None):
             return sb.tile(shape, dtype, name=name, tag=tag or name, align_bytes=64)
 
-        shared = tile("shared", [P, 8192], BF16)
+        wide = {k: tile("a_wide%d" % k, [P, PACK, 2 * SPAN], BF16) for k in (1, 2)}
         a_raw = [
-            [shared[:, 2048 * k : 2048 * (k + 1)].rearrange("p (j c) -> p j c", j=PACK) for k in range(PASSES)],
-            [tile("a_raw1_%d" % k, [P, PACK, SPAN], BF16)[:] for k in range(PASSES)],
-            [tile("a_raw2_%d" % k, [P, PACK, SPAN], BF16)[:] for k in range(PASSES)],
+            [
+                wide[k][:, :, g * SPAN : (g + 1) * SPAN]
+                if g < 2 and k in wide
+                else tile("a_raw%d_%d" % (g, k), [P, PACK, SPAN], BF16)[:]
+                for k in range(PASSES)
+            ]
+            for g in range(GROUPS)
         ]
         stage = [tile("a_stage%d" % i, [P, SPAN * PACK], BF16) for i in range(STAGES)]
         stage_index = {}
         a_codes = [[tile("a_codes%d_%d" % (g, k), [P, SPAN], U32) for k in range(PASSES)] for g in range(GROUPS)]
         a_scales = [[tile("a_scales%d_%d" % (g, k), [P, SPAN], U8) for k in range(PASSES)] for g in range(GROUPS)]
         v_codes = [tile("v_codes%d" % h, [P, PASSES, HALF], U32) for h in range(2)]
-        v_plane = [tile("v_plane%d" % h, [P, PASSES, HALF], U8) for h in range(2)]
+        v_plane = tile("v_plane", [P, PASSES, NB], U8)
         xc = [tile("xc%d" % g, [P, 2, PACK, NB], BF16) for g in range(2)]
-        x_sb = [xc[0][:, 0], xc[1][:, 0], shared[:, 0:4096].rearrange("p (t m) -> p t m", t=PACK)]
-        c_sb = [xc[0][:, 1], xc[1][:, 1], shared[:, 4096:8192].rearrange("p (t m) -> p t m", t=PACK)]
+        x_sb = [xc[0][:, 0], xc[1][:, 0], wide[1][:]]
+        c_sb = [xc[0][:, 1], xc[1][:, 1], wide[2][:]]
         y = [tile("y%d" % g, [P, PACK, NB], F32) for g in range(2)]
         y_bf = [tile("y_bf%d" % g, [P, NB * PACK], BF16) for g in range(GROUPS)]
         y_codes = [tile("y_codes%d" % g, [P, NB], U32) for g in range(GROUPS)]
-        y_plane = tile("y_plane", [P, GROUPS, NB], U8)
+        y_early = tile("y_plane_early", [P, GROUPS - 1, NB], U8)
+        y_last = tile("y_plane_last", [P, 1, NB], U8)
+        y_plane = [y_early[:, 0, :], y_early[:, 1, :], y_last[:, 0, :]]
         d_bf = tile("d_bf", [P, GROUPS, 16], BF16)
         sigma_bf = tile("sigma_bf", [P, GROUPS, 16], BF16)
         sigma_f = tile("sigma_f", [P, GROUPS, PACK], F32)
@@ -64,7 +70,7 @@ def tile_splitting_qp_kkt_rhs_k2_kernel(tc, v_words, v_scales, a, c, d, sigma, x
 
         def load_a(g0, g1, k):
             src = a[k * SPAN : (k + 1) * SPAN, g0 * SPAN : g1 * SPAN].rearrange("(p j) c -> p j c", j=PACK)
-            nc.sync.dma_start(out=a_raw[g0][k], in_=src)
+            nc.sync.dma_start(out=a_raw[g0][k] if g1 == g0 + 1 else wide[k][:], in_=src)
 
         v_bytes = v_words.rearrange("k p n t -> p k (n t)")
 
@@ -72,13 +78,10 @@ def tile_splitting_qp_kkt_rhs_k2_kernel(tc, v_words, v_scales, a, c, d, sigma, x
             src = v_bytes[:, k0:k1, h * HALF * PACK : (h + 1) * HALF * PACK].bitcast(I32)
             nc.sync.dma_start(out=v_codes[h][:, k0:k1, :].bitcast(I32), in_=src)
 
-        def load_v_scales(h):
+        def load_v_scales():
             src = v_scales.rearrange("k (q r) n -> r q k n", r=4)
             for r in range(4):
-                nc.sync.dma_start(
-                    out=v_plane[h][r:P:32, :, :].bitcast(I32),
-                    in_=src[r][:, :, h * HALF : (h + 1) * HALF].bitcast(I32),
-                )
+                nc.sync.dma_start(out=v_plane[r:P:32, :, :].bitcast(I32), in_=src[r].bitcast(I32))
 
         def load_x(g, t0, t1, m0, m1):
             nc.sync.dma_start(out=x_sb[g][:, t0:t1, m0:m1], in_=rows(x, g)[:, t0:t1, m0:m1])
@@ -113,7 +116,7 @@ def tile_splitting_qp_kkt_rhs_k2_kernel(tc, v_words, v_scales, a, c, d, sigma, x
                 lhsT=a_codes[g][k][:, cols].bitcast(E4M3X4),
                 lhsT_scale=a_scales[g][k][:, cols],
                 rhs=v_codes[h][:, k, :].bitcast(E5M2X4),
-                rhs_scale=v_plane[h][:, k, :],
+                rhs_scale=v_plane[:, k, h * HALF : (h + 1) * HALF],
                 start=(k == 0),
                 stop=(k == PASSES - 1),
             )
@@ -160,7 +163,7 @@ def tile_splitting_qp_kkt_rhs_k2_kernel(tc, v_words, v_scales, a, c, d, sigma, x
 
         def quantize_y(g, m0, m1):
             nc.vector.quantize_mx(
-                out=y_codes[g][:, m0:m1].bitcast(E4M3X4), scales=y_plane[:, g, m0:m1], in_=y_stage(g, m0, m1)
+                out=y_codes[g][:, m0:m1].bitcast(E4M3X4), scales=y_plane[g][:, m0:m1], in_=y_stage(g, m0, m1)
             )
 
         def store_y(g, m0, m1):
@@ -173,7 +176,7 @@ def tile_splitting_qp_kkt_rhs_k2_kernel(tc, v_words, v_scales, a, c, d, sigma, x
         def store_scales(g0, g1, queue):
             dst = out_2[g0:g1].rearrange("g (q r) m -> r q g m", r=4)
             for r in range(4):
-                queue.dma_start(out=dst[r].bitcast(I32), in_=y_plane[r:P:32, g0:g1, :].bitcast(I32))
+                queue.dma_start(out=dst[r].bitcast(I32), in_=(y_early if g0 == 0 else y_last)[r:P:32, :, :].bitcast(I32))
 
         def each_t(step, first, *rest):
             for t in range(PACK):
@@ -185,16 +188,16 @@ def tile_splitting_qp_kkt_rhs_k2_kernel(tc, v_words, v_scales, a, c, d, sigma, x
 
         ctx.enter_context(tc.manual_schedule())
 
-        for h in range(2):
-            nc.vector.memset(v_plane[h][:].bitcast(U32), 0)
+        nc.vector.memset(v_plane[:].bitcast(U32), 0)
         nc.scalar.dma_start(out=sigma_bf[:, :, 0:PACK], in_=sigma.rearrange("(g p t) -> p g t", p=P, t=PACK))
         nc.scalar.activation(out=sigma_f[:], in_=sigma_bf[:, :, 0:PACK], func=COPY)
 
         load_a(0, 1, 0)
-        load_a(0, 1, 1)
-        load_v_scales(0)
+        load_a(1, 2, 0)
+        load_a(0, 2, 1)
+        load_v_scales()
+        load_a(0, 2, 2)
         load_v(0, 0, 2)
-        load_a(0, 1, 2)
         load_a(0, 1, 3)
         nc.sync.dma_start(out=d_bf[:, :, 0:PACK], in_=d.rearrange("(g p t) -> p g t", p=P, t=PACK))
         load_x(0, 0, 2, 0, NB)
@@ -202,24 +205,23 @@ def tile_splitting_qp_kkt_rhs_k2_kernel(tc, v_words, v_scales, a, c, d, sigma, x
         load_v(0, 2, 4)
         load_x(0, 2, 4, 0, NB)
         load_c(0, 2, 4, 0, NB)
-        load_v_scales(1)
         load_v(1, 0, 2)
         load_x(1, 0, 2, 0, NB)
         load_v(1, 2, 4)
-        load_a(1, 2, 0)
-        load_a(1, 2, 1)
-        load_c(1, 0, 2, 0, NB)
-        load_a(1, 2, 2)
         load_a(1, 2, 3)
+        load_c(1, 0, 2, 0, NB)
         load_x(1, 2, 4, 0, NB)
         load_c(1, 2, 4, 0, NB)
 
-        for k in range(PASSES):
-            lay_a(0, k, 1, SCALAR)
-            lay_a(0, k, 0, VECTOR)
-            if k >= 1:
-                quantize_a(0, k - 1)
-        quantize_a(0, PASSES - 1)
+        for k in range(PASSES - 1):
+            for g in range(2):
+                lay_a(g, k, 1, SCALAR)
+                lay_a(g, k, 0, VECTOR)
+            quantize_a(0, k)
+            quantize_a(1, k)
+        lay_a(0, 3, 1, SCALAR)
+        lay_a(0, 3, 0, VECTOR)
+        quantize_a(0, 3)
         load_a(2, 3, 0)
         load_x(2, 0, 4, 0, NB)
         load_a(2, 3, 1)
@@ -245,76 +247,71 @@ def tile_splitting_qp_kkt_rhs_k2_kernel(tc, v_words, v_scales, a, c, d, sigma, x
         add_cost(0, 3, 0, NB)
         add_product(0, 2, 0, HALF)
         add_product(0, 3, 0, HALF)
+        each_t(add_product, 0, HALF, NB)
         scale_x(1, 0, 0, NB)
         scale_x(1, 1, 0, NB)
-        each_t(add_product, 0, HALF, NB)
-        lay_a(1, 0, 1, SCALAR)
-        lay_a(1, 0, 0, SCALAR)
-        lay_a(1, 1, 1, SCALAR)
-        lay_a(1, 1, 0, VECTOR)
-        quantize_a(1, 0)
-        add_cost(1, 0, 0, NB)
-        quantize_a(1, 1)
-        lay_a(1, 2, 1, SCALAR)
-        lay_a(1, 2, 0, SCALAR)
-        add_cost(1, 1, 0, NB)
         lay_a(1, 3, 1, SCALAR)
-        lay_a(1, 3, 0, VECTOR)
-        quantize_a(1, 2)
-        quantize_a(1, 3)
-        for k in range(PASSES - 1):
-            for h in range(2):
-                each_t(lambda h, t: multiply(1, h, t, k), h)
-        for h in range(2):
-            each_t(lambda h, t: multiply(1, h, t, 3), h)
+        lay_a(1, 3, 0, SCALAR)
         scale_x(1, 2, 0, NB)
         scale_x(1, 3, 0, NB)
-        add_cost(1, 2, 0, NB)
-        add_cost(1, 3, 0, NB)
+        add_cost(1, 0, 0, NB)
+        quantize_a(1, 3)
+        for t in range(1, PACK):
+            add_cost(1, t, 0, NB)
+        for h in range(2):
+            for t in range(PACK):
+                for k in range(PASSES - 1):
+                    multiply(1, h, t, k)
+            for t in (0, 1, 3, 2):
+                multiply(1, h, t, 3)
         each_t(scale_x, 2, 0, NB, GPSIMD)
-        each_t(add_product, 1, 0, HALF)
+        for t in (2, 0, 1, 3):
+            add_product(1, t, 0, HALF)
         store_y(0, 0, NB)
-        last_first(add_product, 1, HALF, NB)
-        store_y(1, 0, HALF)
-        store_y(1, HALF, NB)
-        for k in range(4):
+        for t in (2, 0, 1, 3):
+            add_product(1, t, HALF, NB)
+        store_y(1, 0, NB)
+        lay_a(2, 0, 1, SCALAR)
+        lay_a(2, 0, 0, SCALAR)
+        lay_y(0, 0, HALF, SCALAR)
+        for k in range(1, PASSES):
             lay_a(2, k, 1, SCALAR)
             lay_a(2, k, 0, SCALAR)
         quantize_a(2, 0)
         quantize_a(2, 1)
-        quantize_a(2, 2)
+        quantize_y(0, 0, HALF)
+        store_codes(0, 0, HALF)
         add_cost(2, 0, 0, HALF)
-        quantize_a(2, 3)
+        quantize_a(2, 2)
         add_cost(2, 1, 0, HALF)
         add_cost(2, 2, 0, HALF)
+        quantize_a(2, 3)
         add_cost(2, 3, 0, HALF)
-        for k in range(3):
-            each_t(lambda h, t: multiply(2, h, t, k), 0)
-        last_first(lambda h, t: multiply(2, h, t, 3), 0)
-        for t in (3, 0, 1, 2):
+        add_cost(2, 0, HALF, NB)
+        for k in range(PASSES):
+            last_first(lambda h, t: multiply(2, h, t, k), 0)
+        for t in range(PACK):
             for k in range(PASSES):
                 multiply(2, 1, t, k)
-        lay_y(0, 0, HALF, SCALAR)
         lay_y(0, HALF, NB, SCALAR)
         lay_y(1, 0, HALF, SCALAR)
-        quantize_y(0, 0, HALF)
         lay_y(1, HALF, NB, SCALAR)
         last_first(add_product, 2, 0, HALF)
         store_y(2, 0, HALF)
-        quantize_y(0, HALF, NB)
-        store_codes(0, 0, NB)
         lay_y(2, 0, HALF, SCALAR)
-        add_cost(2, 0, HALF, NB)
+        quantize_y(0, HALF, NB)
+        store_codes(0, HALF, NB)
         add_cost(2, 1, HALF, NB)
-        quantize_y(1, 0, HALF)
         add_cost(2, 2, HALF, NB)
         add_cost(2, 3, HALF, NB)
-        quantize_y(1, HALF, NB)
-        store_codes(1, 0, NB)
-        store_scales(0, 2, nc.sync)
+        quantize_y(1, 0, HALF)
+        store_codes(1, 0, HALF)
         last_first(add_product, 2, HALF, HALF + QUARTER)
         store_y(2, HALF, HALF + QUARTER)
         lay_y(2, HALF, HALF + QUARTER, SCALAR)
+        quantize_y(1, HALF, NB)
+        store_codes(1, HALF, NB)
+        store_scales(0, 2, nc.sync)
         each_t(add_product, 2, HALF + QUARTER, NB)
         store_y(2, HALF + QUARTER, NB)
         quantize_y(2, 0, HALF)
@@ -323,4 +320,4 @@ def tile_splitting_qp_kkt_rhs_k2_kernel(tc, v_words, v_scales, a, c, d, sigma, x
         quantize_y(2, HALF, HALF + QUARTER)
         quantize_y(2, HALF + QUARTER, NB)
         store_codes(2, HALF, NB)
-        store_scales(2, 3, nc.scalar)
+        store_scales(2, 3, nc.sync)

@@ -166,8 +166,8 @@ def tile_splitting_qp_kkt_rhs_k2_kernel(tc, v_words, v_scales, a, c, d, sigma, x
                 out=y_codes[g][:, m0:m1].bitcast(E4M3X4), scales=y_plane[g][:, m0:m1], in_=y_stage(g, m0, m1)
             )
 
-        def store_y(g, m0, m1):
-            nc.sync.dma_start(out=rows(out_0, g)[:, :, m0:m1], in_=y_part(g, m0, m1))
+        def store_y(g, m0, m1, t0=0, t1=PACK):
+            nc.sync.dma_start(out=rows(out_0, g)[:, t0:t1, m0:m1], in_=y_part(g, m0, m1)[:, t0:t1, :])
 
         def store_codes(g, m0, m1):
             dst = out_1[g].rearrange("p m t -> p (m t)")[:, m0 * PACK : m1 * PACK].bitcast(I32)
@@ -195,16 +195,16 @@ def tile_splitting_qp_kkt_rhs_k2_kernel(tc, v_words, v_scales, a, c, d, sigma, x
         load_a(0, 1, 0)
         load_a(1, 2, 0)
         load_a(0, 2, 1)
-        load_v_scales()
         load_a(0, 2, 2)
-        load_v(0, 0, 2)
+        load_x(0, 0, 2, 0, NB)
+        load_v_scales()
         load_a(0, 1, 3)
         nc.sync.dma_start(out=d_bf[:, :, 0:PACK], in_=d.rearrange("(g p t) -> p g t", p=P, t=PACK))
-        load_x(0, 0, 2, 0, NB)
         load_c(0, 0, 2, 0, NB)
-        load_v(0, 2, 4)
+        load_v(0, 0, 2)
         load_x(0, 2, 4, 0, NB)
         load_c(0, 2, 4, 0, NB)
+        load_v(0, 2, 4)
         load_v(1, 0, 2)
         load_x(1, 0, 2, 0, NB)
         load_v(1, 2, 4)
@@ -219,99 +219,98 @@ def tile_splitting_qp_kkt_rhs_k2_kernel(tc, v_words, v_scales, a, c, d, sigma, x
                 lay_a(g, k, 0, VECTOR)
             quantize_a(0, k)
             quantize_a(1, k)
+        load_x(2, 0, 4, 0, NB)
+        for k in range(PASSES - 1):
+            load_a(2, 3, k)
+        load_c(2, 0, 4, 0, NB)
+        load_a(2, 3, 3)
+        scale_x(0, 0, 0, NB)
         lay_a(0, 3, 1, SCALAR)
         lay_a(0, 3, 0, VECTOR)
-        quantize_a(0, 3)
-        load_a(2, 3, 0)
-        load_x(2, 0, 4, 0, NB)
-        load_a(2, 3, 1)
-        load_a(2, 3, 2)
-        load_a(2, 3, 3)
-        load_c(2, 0, 4, 0, NB)
-        for k in range(2):
-            each_t(lambda h, t: multiply(0, h, t, k), 0)
-        for t in range(PACK):
-            for k in range(2, PASSES):
-                multiply(0, 0, t, k)
-        for k in range(2):
-            each_t(lambda h, t: multiply(0, h, t, k), 1)
-        for t in range(PACK):
-            for k in range(2, PASSES):
-                multiply(0, 1, t, k)
-        each_t(scale_x, 0, 0, NB)
         add_cost(0, 0, 0, NB)
-        add_cost(0, 1, 0, NB)
-        add_product(0, 0, 0, HALF)
-        add_product(0, 1, 0, HALF)
-        add_cost(0, 2, 0, NB)
-        add_cost(0, 3, 0, NB)
-        add_product(0, 2, 0, HALF)
-        add_product(0, 3, 0, HALF)
-        each_t(add_product, 0, HALF, NB)
+        quantize_a(0, 3)
+        for t in range(1, PACK):
+            scale_x(0, t, 0, NB)
+            add_cost(0, t, 0, NB)
+        for h, ts in ((0, (0, 1, 2, 3)), (1, (0, 1)), (1, (2, 3))):
+            for ks in ((0, 1), (2, 3)):
+                for t in ts:
+                    for k in ks:
+                        multiply(0, h, t, k)
+        each_t(add_product, 0, 0, HALF)
+        add_product(0, 0, HALF, NB)
+        add_product(0, 1, HALF, NB)
+
         scale_x(1, 0, 0, NB)
         scale_x(1, 1, 0, NB)
         lay_a(1, 3, 1, SCALAR)
         lay_a(1, 3, 0, SCALAR)
         scale_x(1, 2, 0, NB)
         scale_x(1, 3, 0, NB)
-        add_cost(1, 0, 0, NB)
-        quantize_a(1, 3)
-        for t in range(1, PACK):
-            add_cost(1, t, 0, NB)
-        for h in range(2):
-            for t in range(PACK):
-                for k in range(PASSES - 1):
-                    multiply(1, h, t, k)
-            for t in (0, 1, 3, 2):
-                multiply(1, h, t, 3)
-        each_t(scale_x, 2, 0, NB, GPSIMD)
-        for t in (2, 0, 1, 3):
-            add_product(1, t, 0, HALF)
-        store_y(0, 0, NB)
-        for t in (2, 0, 1, 3):
-            add_product(1, t, HALF, NB)
-        store_y(1, 0, NB)
-        lay_a(2, 0, 1, SCALAR)
-        lay_a(2, 0, 0, SCALAR)
         lay_y(0, 0, HALF, SCALAR)
-        for k in range(1, PASSES):
+        add_cost(1, 0, 0, NB)
+        add_cost(1, 1, 0, NB)
+        quantize_a(1, 3)
+        add_cost(1, 2, 0, NB)
+        add_cost(1, 3, 0, NB)
+        each_t(scale_x, 2, 0, NB, GPSIMD)
+        for t in range(PACK):
+            for k in range(PASSES - 1):
+                multiply(1, 0, t, k)
+        each_t(lambda h, t: multiply(1, h, t, 3), 0)
+        add_product(1, 2, 0, HALF)
+        add_product(1, 0, 0, HALF)
+        add_product(0, 2, HALF, NB)
+        add_product(0, 3, HALF, NB)
+        add_product(1, 1, 0, HALF)
+        add_product(1, 3, 0, HALF)
+        store_y(0, 0, NB)
+        for t in range(PACK):
+            for k in range(PASSES):
+                multiply(1, 1, t, k)
+        each_t(add_product, 1, HALF, NB)
+        for k in range(PASSES):
             lay_a(2, k, 1, SCALAR)
             lay_a(2, k, 0, SCALAR)
         quantize_a(2, 0)
-        quantize_a(2, 1)
         quantize_y(0, 0, HALF)
         store_codes(0, 0, HALF)
-        add_cost(2, 0, 0, HALF)
+        store_y(1, 0, NB)
+        quantize_a(2, 1)
         quantize_a(2, 2)
+        add_cost(2, 0, 0, HALF)
         add_cost(2, 1, 0, HALF)
         add_cost(2, 2, 0, HALF)
         quantize_a(2, 3)
         add_cost(2, 3, 0, HALF)
         add_cost(2, 0, HALF, NB)
         for k in range(PASSES):
-            last_first(lambda h, t: multiply(2, h, t, k), 0)
+            for t in (2, 3, 0, 1):
+                multiply(2, 0, t, k)
         for t in range(PACK):
             for k in range(PASSES):
                 multiply(2, 1, t, k)
         lay_y(0, HALF, NB, SCALAR)
         lay_y(1, 0, HALF, SCALAR)
         lay_y(1, HALF, NB, SCALAR)
-        last_first(add_product, 2, 0, HALF)
-        store_y(2, 0, HALF)
+        for t in (2, 3, 0, 1):
+            add_product(2, t, 0, HALF)
+        store_y(2, 0, HALF, 2, 4)
+        store_y(2, 0, HALF, 0, 2)
         lay_y(2, 0, HALF, SCALAR)
         quantize_y(0, HALF, NB)
         store_codes(0, HALF, NB)
         add_cost(2, 1, HALF, NB)
         add_cost(2, 2, HALF, NB)
-        add_cost(2, 3, HALF, NB)
         quantize_y(1, 0, HALF)
         store_codes(1, 0, HALF)
-        last_first(add_product, 2, HALF, HALF + QUARTER)
-        store_y(2, HALF, HALF + QUARTER)
-        lay_y(2, HALF, HALF + QUARTER, SCALAR)
+        add_cost(2, 3, HALF, NB)
         quantize_y(1, HALF, NB)
         store_codes(1, HALF, NB)
         store_scales(0, 2, nc.sync)
+        last_first(add_product, 2, HALF, HALF + QUARTER)
+        store_y(2, HALF, HALF + QUARTER)
+        lay_y(2, HALF, HALF + QUARTER, SCALAR)
         each_t(add_product, 2, HALF + QUARTER, NB)
         store_y(2, HALF + QUARTER, NB)
         quantize_y(2, 0, HALF)

from contextlib import ExitStack

import concourse.mybir as mybir

NC, NV, NB = 2048, 1536, 1024
FLOPS = 2 * NC * NV * NB

F32 = mybir.dt.float32
BF16 = mybir.dt.bfloat16
I32 = mybir.dt.int32
U32 = mybir.dt.uint32
U8 = mybir.dt.uint8
E4M3X4 = mybir.dt.float8_e4m3fn_x4
E5M2X4 = mybir.dt.float8_e5m2_x4
ALU = mybir.AluOpType
COPY = mybir.ActivationFunctionType.Copy

P = 128
PACK = 4
SPAN = P * PACK
PASSES = NC // SPAN
GROUPS = NV // SPAN
HALF = 512
QUARTER = 256
STAGES = 6
VECTOR, SCALAR, GPSIMD = "vector", "scalar", "gpsimd"


def tile_splitting_qp_kkt_rhs_k2_kernel(tc, v_words, v_scales, a, c, d, sigma, x, out_0, out_1, out_2):
    nc = tc.nc
    with ExitStack() as ctx:
        sb = ctx.enter_context(tc.tile_pool(name="sb", bufs=1))
        ps = ctx.enter_context(tc.psum_pool(name="ps", bufs=1))

        def tile(name, shape, dtype, tag=None):
            return sb.tile(shape, dtype, name=name, tag=tag or name, align_bytes=64)

        wide = {k: tile("a_wide%d" % k, [P, PACK, 2 * SPAN], BF16) for k in (1, 2)}
        a_raw = [
            [
                wide[k][:, :, g * SPAN : (g + 1) * SPAN]
                if g < 2 and k in wide
                else tile("a_raw%d_%d" % (g, k), [P, PACK, SPAN], BF16)[:]
                for k in range(PASSES)
            ]
            for g in range(GROUPS)
        ]
        stage = [tile("a_stage%d" % i, [P, SPAN * PACK], BF16) for i in range(STAGES)]
        stage_index = {}
        a_codes = [[tile("a_codes%d_%d" % (g, k), [P, SPAN], U32) for k in range(PASSES)] for g in range(GROUPS)]
        a_scales = [[tile("a_scales%d_%d" % (g, k), [P, SPAN], U8) for k in range(PASSES)] for g in range(GROUPS)]
        v_codes = [tile("v_codes%d" % h, [P, PASSES, HALF], U32) for h in range(2)]
        v_plane = tile("v_plane", [P, PASSES, NB], U8)
        xc = [tile("xc%d" % g, [P, 2, PACK, NB], BF16) for g in range(2)]
        x_sb = [xc[0][:, 0], xc[1][:, 0], wide[1][:]]
        c_sb = [xc[0][:, 1], xc[1][:, 1], wide[2][:]]
        y = [tile("y%d" % g, [P, PACK, NB], F32) for g in range(2)]
        y_bf = [tile("y_bf%d" % g, [P, NB * PACK], BF16) for g in range(GROUPS)]
        y_codes = [tile("y_codes%d" % g, [P, NB], U32) for g in range(GROUPS)]
        y_early = tile("y_plane_early", [P, GROUPS - 1, NB], U8)
        y_last = tile("y_plane_last", [P, 1, NB], U8)
        y_plane = [y_early[:, 0, :], y_early[:, 1, :], y_last[:, 0, :]]
        d_bf = tile("d_bf", [P, GROUPS, 16], BF16)
        sigma_bf = tile("sigma_bf", [P, GROUPS, 16], BF16)
        sigma_f = tile("sigma_f", [P, GROUPS, PACK], F32)
        bank = [[ps.tile([P, HALF], F32, name="bank%d_%d" % (h, t)) for t in range(PACK)] for h in range(2)]

        def rows(ap, g):
            return ap[g * SPAN : (g + 1) * SPAN, :].rearrange("(p t) m -> p t m", t=PACK)

        def load_a(g0, g1, k):
            src = a[k * SPAN : (k + 1) * SPAN, g0 * SPAN : g1 * SPAN].rearrange("(p j) c -> p j c", j=PACK)
            nc.sync.dma_start(out=a_raw[g0][k] if g1 == g0 + 1 else wide[k][:], in_=src)

        v_bytes = v_words.rearrange("k p n t -> p k (n t)")

        def load_v(h, k0, k1):
            src = v_bytes[:, k0:k1, h * HALF * PACK : (h + 1) * HALF * PACK].bitcast(I32)
            nc.sync.dma_start(out=v_codes[h][:, k0:k1, :].bitcast(I32), in_=src)

        def load_v_scales():
            src = v_scales.rearrange("k (q r) n -> r q k n", r=4)
            for r in range(4):
                nc.sync.dma_start(out=v_plane[r:P:32, :, :].bitcast(I32), in_=src[r].bitcast(I32))

        def load_x(g, t0, t1, m0, m1):
            nc.sync.dma_start(out=x_sb[g][:, t0:t1, m0:m1], in_=rows(x, g)[:, t0:t1, m0:m1])

        def load_c(g, t0, t1, m0, m1):
            nc.sync.dma_start(out=c_sb[g][:, t0:t1, m0:m1], in_=rows(c, g)[:, t0:t1, m0:m1])

        def copy(engine, dst, src):
            if engine == VECTOR:
                nc.vector.tensor_copy(out=dst, in_=src)
            else:
                nc.scalar.copy(out=dst, in_=src)

        def stage_of(g, k):
            return stage[stage_index.setdefault((g, k), len(stage_index) % STAGES)]

        def lay_a(g, k, pair, engine):
            src = a_raw[g][k].rearrange("p j (u i t) -> p u j i t", i=2, t=PACK)
            dst = stage_of(g, k)[:].rearrange("p (t u i j) -> p u j i t", t=PACK, i=2, j=PACK)
            ts = slice(2 * pair, 2 * pair + 2)
            copy(engine, dst[:, :, :, :, ts], src[:, :, :, :, ts])

        def quantize_a(g, k):
            nc.vector.quantize_mx(
                out=a_codes[g][k][:].bitcast(E4M3X4), scales=a_scales[g][k][:], in_=stage_of(g, k)[:]
            )

        def multiply(g, h, t, k):
            cols = slice(t * P, (t + 1) * P)
            nc.tensor.matmul_mx(
                out=bank[h][t][:],
                lhsT=a_codes[g][k][:, cols].bitcast(E4M3X4),
                lhsT_scale=a_scales[g][k][:, cols],
                rhs=v_codes[h][:, k, :].bitcast(E5M2X4),
                rhs_scale=v_plane[:, k, h * HALF : (h + 1) * HALF],
                start=(k == 0),
                stop=(k == PASSES - 1),
            )

        def y_part(g, m0, m1):
            if g < 2:
                return y[g][:, :, m0:m1]
            h = m0 // HALF
            return y[g][:, h, :, m0 - h * HALF : m1 - h * HALF]

        def scale_x(g, t, m0, m1, engine=SCALAR):
            if g == len(y):
                y.append(tile("y%d" % g, [P, 2, PACK, HALF], F32, tag="xc1"))
            if engine == SCALAR:
                nc.scalar.activation(
                    out=y_part(g, m0, m1)[:, t, :], in_=x_sb[g][:, t, m0:m1], func=COPY, scale=sigma_f[:, g, t : t + 1]
                )
            else:
                nc.gpsimd.tensor_scalar(
                    out=y[g][:, :, t, :], in0=x_sb[g][:, t, :].rearrange("p (h m) -> p h m", h=2), scalar1=sigma_f[:, g, t : t + 1],
                    scalar2=0.0, op0=ALU.mult, op1=ALU.add,
                )

        def add_cost(g, t, m0, m1):
            nc.vector.scalar_tensor_tensor(
                out=y_part(g, m0, m1)[:, t, :], in0=c_sb[g][:, t, m0:m1], scalar=d_bf[:, g, t : t + 1],
                in1=y_part(g, m0, m1)[:, t, :], op0=ALU.mult, op1=ALU.subtract,
            )

        def add_product(g, t, m0, m1):
            h = m0 // HALF
            nc.vector.scalar_tensor_tensor(
                out=y_part(g, m0, m1)[:, t, :], in0=bank[h][t][:, m0 - h * HALF : m1 - h * HALF],
                scalar=d_bf[:, g, t : t + 1], in1=y_part(g, m0, m1)[:, t, :], op0=ALU.mult, op1=ALU.subtract,
            )

        def y_stage(g, m0, m1):
            return y_bf[g][:, m0 * PACK : m1 * PACK]

        def lay_y(g, m0, m1, engine):
            src = y_part(g, m0, m1).rearrange("p t (u i) -> p u t i", i=4)
            dst = y_stage(g, m0, m1).rearrange("p (u i t) -> p u t i", i=4, t=PACK)
            copy(engine, dst, src)

        def quantize_y(g, m0, m1):
            nc.vector.quantize_mx(
                out=y_codes[g][:, m0:m1].bitcast(E4M3X4), scales=y_plane[g][:, m0:m1], in_=y_stage(g, m0, m1)
            )

        def store_y(g, m0, m1, t0=0, t1=PACK):
            nc.sync.dma_start(out=rows(out_0, g)[:, t0:t1, m0:m1], in_=y_part(g, m0, m1)[:, t0:t1, :])

        def store_codes(g, m0, m1):
            dst = out_1[g].rearrange("p m t -> p (m t)")[:, m0 * PACK : m1 * PACK].bitcast(I32)
            nc.sync.dma_start(out=dst, in_=y_codes[g][:, m0:m1].bitcast(I32))

        def store_scales(g0, g1, queue):
            dst = out_2[g0:g1].rearrange("g (q r) m -> r q g m", r=4)
            for r in range(4):
                queue.dma_start(out=dst[r].bitcast(I32), in_=(y_early if g0 == 0 else y_last)[r:P:32, :, :].bitcast(I32))

        def each_t(step, first, *rest):
            for t in range(PACK):
                step(first, t, *rest)

        def last_first(step, first, *rest):
            for t in (3, 0, 1, 2):
                step(first, t, *rest)

        ctx.enter_context(tc.manual_schedule())

        nc.vector.memset(v_plane[:].bitcast(U32), 0)
        nc.scalar.dma_start(out=sigma_bf[:, :, 0:PACK], in_=sigma.rearrange("(g p t) -> p g t", p=P, t=PACK))
        nc.scalar.activation(out=sigma_f[:], in_=sigma_bf[:, :, 0:PACK], func=COPY)

        load_a(0, 1, 0)
        load_a(1, 2, 0)
        load_a(0, 2, 1)
        load_a(0, 2, 2)
        load_x(0, 0, 2, 0, NB)
        load_v_scales()
        load_a(0, 1, 3)
        nc.sync.dma_start(out=d_bf[:, :, 0:PACK], in_=d.rearrange("(g p t) -> p g t", p=P, t=PACK))
        load_c(0, 0, 2, 0, NB)
        load_v(0, 0, 2)
        load_x(0, 2, 4, 0, NB)
        load_c(0, 2, 4, 0, NB)
        load_v(0, 2, 4)
        load_v(1, 0, 2)
        load_x(1, 0, 2, 0, NB)
        load_v(1, 2, 4)
        load_a(1, 2, 3)
        load_c(1, 0, 2, 0, NB)
        load_x(1, 2, 4, 0, NB)
        load_c(1, 2, 4, 0, NB)

        for k in range(PASSES - 1):
            for g in range(2):
                lay_a(g, k, 1, SCALAR)
                lay_a(g, k, 0, VECTOR)
            quantize_a(0, k)
            quantize_a(1, k)
        load_x(2, 0, 4, 0, NB)
        for k in range(PASSES - 1):
            load_a(2, 3, k)
        load_c(2, 0, 4, 0, NB)
        load_a(2, 3, 3)
        scale_x(0, 0, 0, NB)
        lay_a(0, 3, 1, SCALAR)
        lay_a(0, 3, 0, VECTOR)
        add_cost(0, 0, 0, NB)
        quantize_a(0, 3)
        for t in range(1, PACK):
            scale_x(0, t, 0, NB)
            add_cost(0, t, 0, NB)
        for h, ts in ((0, (0, 1, 2, 3)), (1, (0, 1)), (1, (2, 3))):
            for ks in ((0, 1), (2, 3)):
                for t in ts:
                    for k in ks:
                        multiply(0, h, t, k)
        each_t(add_product, 0, 0, HALF)
        add_product(0, 0, HALF, NB)
        add_product(0, 1, HALF, NB)

        scale_x(1, 0, 0, NB)
        scale_x(1, 1, 0, NB)
        lay_a(1, 3, 1, SCALAR)
        lay_a(1, 3, 0, SCALAR)
        scale_x(1, 2, 0, NB)
        scale_x(1, 3, 0, NB)
        lay_y(0, 0, HALF, SCALAR)
        add_cost(1, 0, 0, NB)
        add_cost(1, 1, 0, NB)
        quantize_a(1, 3)
        add_cost(1, 2, 0, NB)
        add_cost(1, 3, 0, NB)
        each_t(scale_x, 2, 0, NB, GPSIMD)
        for t in range(PACK):
            for k in range(PASSES - 1):
                multiply(1, 0, t, k)
        each_t(lambda h, t: multiply(1, h, t, 3), 0)
        add_product(1, 2, 0, HALF)
        add_product(1, 0, 0, HALF)
        add_product(0, 2, HALF, NB)
        add_product(0, 3, HALF, NB)
        add_product(1, 1, 0, HALF)
        add_product(1, 3, 0, HALF)
        store_y(0, 0, NB)
        for t in range(PACK):
            for k in range(PASSES):
                multiply(1, 1, t, k)
        each_t(add_product, 1, HALF, NB)
        for k in range(PASSES):
            lay_a(2, k, 1, SCALAR)
            lay_a(2, k, 0, SCALAR)
        quantize_a(2, 0)
        quantize_y(0, 0, HALF)
        store_codes(0, 0, HALF)
        store_y(1, 0, NB)
        quantize_a(2, 1)
        quantize_a(2, 2)
        add_cost(2, 0, 0, HALF)
        add_cost(2, 1, 0, HALF)
        add_cost(2, 2, 0, HALF)
        quantize_a(2, 3)
        add_cost(2, 3, 0, HALF)
        add_cost(2, 0, HALF, NB)
        for k in range(PASSES):
            for t in (2, 3, 0, 1):
                multiply(2, 0, t, k)
        for t in range(PACK):
            for k in range(PASSES):
                multiply(2, 1, t, k)
        lay_y(0, HALF, NB, SCALAR)
        lay_y(1, 0, HALF, SCALAR)
        lay_y(1, HALF, NB, SCALAR)
        for t in (2, 3, 0, 1):
            add_product(2, t, 0, HALF)
        store_y(2, 0, HALF, 2, 4)
        store_y(2, 0, HALF, 0, 2)
        lay_y(2, 0, HALF, SCALAR)
        quantize_y(0, HALF, NB)
        store_codes(0, HALF, NB)
        add_cost(2, 1, HALF, NB)
        add_cost(2, 2, HALF, NB)
        quantize_y(1, 0, HALF)
        store_codes(1, 0, HALF)
        add_cost(2, 3, HALF, NB)
        quantize_y(1, HALF, NB)
        store_codes(1, HALF, NB)
        store_scales(0, 2, nc.sync)
        last_first(add_product, 2, HALF, HALF + QUARTER)
        store_y(2, HALF, HALF + QUARTER)
        lay_y(2, HALF, HALF + QUARTER, SCALAR)
        each_t(add_product, 2, HALF + QUARTER, NB)
        store_y(2, HALF + QUARTER, NB)
        quantize_y(2, 0, HALF)
        store_codes(2, 0, HALF)
        lay_y(2, HALF + QUARTER, NB, VECTOR)
        quantize_y(2, HALF, HALF + QUARTER)
        quantize_y(2, HALF + QUARTER, NB)
        store_codes(2, HALF, NB)
        store_scales(2, 3, nc.sync)
